import numpy as np
import ml_dtypes


def mxq(x, axis, fmt="e4m3"):
    dtype, down = {"e4m3": (ml_dtypes.float8_e4m3fn, 7), "e5m2": (ml_dtypes.float8_e5m2, 14)}[fmt]
    v = np.moveaxis(np.asarray(x, np.float32).astype(ml_dtypes.bfloat16).astype(np.float64), axis, -1)
    blocks = v.reshape(v.shape[:-1] + (-1, 32))
    amax = np.abs(blocks).max(-1, keepdims=True)
    byte = np.maximum(np.where(amax > 0, np.frexp(amax)[1] - 1 + 127, 0) - down, 1)
    scale = np.exp2(byte - 127.0)
    codes = (blocks / scale).astype(np.float32).astype(dtype).astype(np.float64)
    return np.moveaxis((codes * scale).reshape(v.shape), -1, axis)


WIDE = False


def mx_kscale(k):
    if not WIDE:
        return np.ones(k)
    levels = np.array([10, -10, 5, -5, 0])
    if k % 512:
        return np.exp2(np.random.permutation(np.resize(levels, k // 32))).repeat(32)
    a = np.empty((k // 512, 16))
    for p in range(k // 512):
        a[p, :8] = np.random.permutation(np.resize(levels, 8))
        for g in range(8):
            far = levels[np.abs(levels - a[p, g]) >= 10]
            a[p, g + 8] = far[np.random.randint(len(far))]
    return np.exp2(a.ravel()).repeat(32)


def f64(x):
    return np.asarray(x).astype(np.float64)


def striped(idx):
    return np.tile(idx.reshape(-1, 16).T, (8, 1)).astype(np.uint16)


def unstriped(offs):
    return offs[:16].T.reshape(-1).astype(np.int64)


E2M1 = np.array([0.0, 0.5, 1.0, 1.5, 2.0, 3.0, 4.0, 6.0, -0.0, -0.5, -1.0, -1.5, -2.0, -3.0, -4.0, -6.0])


def pack_weight(w, fmt):
    k, n = w.shape
    w = f64(np.asarray(w, np.float32).astype(ml_dtypes.bfloat16)).reshape(k // 32, 32, n)
    amax = np.abs(w).max(1)
    if fmt == "e4m3":
        byte = np.frexp(amax)[1] - 1 + 127 - 7
    else:
        mant, ex = np.frexp(amax / 6.0)
        byte = np.where(mant > 0.5, ex, ex - 1) + 127
    byte = np.clip(np.where(amax > 0, byte, 1), 1, 254)
    scaled = (w * np.exp2(127.0 - byte)[:, None, :]).reshape(k, n).astype(np.float32)
    by_word = np.ascontiguousarray(scaled.reshape(k // 512, 128, 4, n).transpose(0, 1, 3, 2))
    if fmt == "e4m3":
        words = by_word.astype(ml_dtypes.float8_e4m3fn).view(np.uint8)
    else:
        c = by_word.astype(ml_dtypes.float4_e2m1fn).view(np.uint8) & 0xF
        words = (c[..., 0::2] | (c[..., 1::2] << 4)).reshape(k // 512, 128, 2 * n)
    return np.ascontiguousarray(words), np.ascontiguousarray(byte.astype(np.uint8).reshape(k // 512, 16, n))


def unpack_weight(words, scales, fmt):
    g, _, n = scales.shape
    words = np.ascontiguousarray(words).reshape(g, 128, n, -1)
    if fmt == "e4m3":
        vals = words.view(ml_dtypes.float8_e4m3fn).astype(np.float64)
    else:
        nib = np.empty((g, 128, n, 4), np.uint8)
        nib[..., 0::2] = words & 0xF
        nib[..., 1::2] = words >> 4
        vals = E2M1[nib]
    vals = vals * np.repeat(np.exp2(scales.astype(np.float64) - 127.0), 8, axis=1)[..., None]
    return vals.transpose(0, 1, 3, 2).reshape(g * 512, n)


def gelu(v):
    return 0.5 * v * (1.0 + np.tanh(np.sqrt(2.0 / np.pi) * (v + 0.044715 * v**3)))


K, H, N, T, S, P, T2 = 1024, 1024, 512, 2048, 1024, 512, 2048

def setup_inputs():
    n = np.random.standard_normal
    s = mx_kscale(K)[:, None]
    u = mx_kscale(H)[:, None]
    perm = np.random.permutation(T2)
    d = {}
    d["tab_words"], d["tab_scales"] = pack_weight(n((K, T)) * s, "e4m3")
    d["tab2_words"], d["tab2_scales"] = pack_weight(n((K, T)) * s, "e4m3")
    d["offs"] = striped(np.random.permutation(T)[:S])
    d["offs2"] = striped(np.random.permutation(T)[:P])
    d["pos1"] = striped(np.random.permutation(S)[:P])
    d["offs3"] = striped(perm[:S])
    d["offs4"] = striped(perm[S:S + P])
    d["w1"] = (0.4 * n((K, H)) / np.sqrt(K) / s).astype(np.float32)
    d["b1"] = np.random.uniform(-0.7, 0.7, H).astype(np.float32)
    d["g1"] = (np.exp(0.3 * n(H)) * u[:, 0]).astype(np.float32)
    d["w2_words"], d["w2_scales"] = pack_weight(n((K, H)) / np.sqrt(K) / s * u.T, "e4m3")
    d["w3_words"], d["w3_scales"] = pack_weight(2.0 * n((H, N)) / np.sqrt(H) / u, "e2m1")
    d["w4"] = (2.0 * n((H, N)) / np.sqrt(H) / u).astype(np.float32)
    d["w5"] = (2.0 * n((H, N)) / np.sqrt(H) / u).astype(np.float32)
    d["wg1"] = np.exp(0.3 * n((128, S))).astype(np.float32)
    d["wg2"] = np.exp(0.3 * n((128, P))).astype(np.float32)
    d["page1"] = n((N, T2)).astype(np.float32)
    return d

def reference(tab_words, tab_scales, tab2_words, tab2_scales, offs, offs2, pos1, offs3, offs4,
              w1, b1, g1, w2_words, w2_scales, w3_words, w3_scales, w4, w5, wg1, wg2, page1):
    v = unpack_weight(tab_words, tab_scales, "e4m3")[:, unstriped(offs)]
    v2 = unpack_weight(tab2_words, tab2_scales, "e4m3")[:, unstriped(offs2)]
    h1 = (mxq(f64(w1), 0, "e4m3").T @ v) + f64(b1)[:, None]
    h2 = unpack_weight(w2_words, w2_scales, "e4m3").T @ v2
    z1 = mxq(f64(g1)[:, None] * np.sin(h1), 0, "e4m3")
    z2 = mxq(h2 * h1[:, unstriped(pos1)], 0, "e4m3")
    y1 = np.maximum(unpack_weight(w3_words, w3_scales, "e2m1").T @ z1, mxq(f64(w4), 0, "e4m3").T @ z1)
    y2 = mxq(f64(w5), 0, "e4m3").T @ z2
    out = f64(page1).copy()
    out[:, unstriped(offs3)] = np.tile(f64(wg1), (N // 128, 1)) * y1
    out[:, unstriped(offs4)] = np.tile(f64(wg2), (N // 128, 1)) * y2
    return out

@@ -1,0 +1,335 @@
+from contextlib import ExitStack
+
+import concourse.mybir as mybir
+
+K, H, N, T, S, L, T2 = 1024, 1024, 512, 2048, 1024, 512, 2048
+FLOPS = 2 * (K * H * S + K * H * L + 2 * H * N * S + H * N * L)
+
+F32 = mybir.dt.float32
+BF16 = mybir.dt.bfloat16
+I32 = mybir.dt.int32
+U32 = mybir.dt.uint32
+U16 = mybir.dt.uint16
+U8 = mybir.dt.uint8
+E4M3 = mybir.dt.float8_e4m3fn_x4
+E2M1 = mybir.dt.float4_e2m1fn_x4
+ACT = mybir.ActivationFunctionType
+MULT = mybir.AluOpType.mult
+MAX = mybir.AluOpType.max
+
+P = 128
+PASSES = 2
+BANK = 512
+
+
+def tile_list_resale_disposition_slots_kernel(
+    tc, tab_words, tab_scales, tab2_words, tab2_scales, offs, offs2, pos1, offs3, offs4,
+    w1, b1, g1, w2_words, w2_scales, w3_words, w3_scales, w4, w5, wg1, wg2, page1, out,
+):
+    nc = tc.nc
+    with ExitStack() as ctx:
+        lists = ctx.enter_context(tc.tile_pool(name="lists", bufs=1))
+        keep = ctx.enter_context(tc.tile_pool(name="keep", bufs=1))
+        work = ctx.enter_context(tc.tile_pool(name="work", bufs=2))
+        psum = ctx.enter_context(tc.psum_pool(name="psum", bufs=8))
+
+        def held(shape, dtype, name):
+            return keep.tile(shape, dtype, name=name, align_bytes=64)
+
+        def rotating(shape, dtype, tag, bufs):
+            return work.tile(shape, dtype, name=tag, tag=tag, bufs=bufs, align_bytes=64)
+
+        def load_list(src, name):
+            tile = lists.tile(list(src.shape), U16, name=name)
+            nc.sync.dma_start(tile[:], src)
+            return tile
+
+        def load_packed_scales(src, name, clear, queue):
+            cols = src.shape[2]
+            plane = held([P, cols], U8, name)
+            clear.memset(plane[:].bitcast(I32), 0)
+            for q in range(4):
+                queue.dma_start(
+                    plane[32 * q : 32 * q + 4 * PASSES, :].bitcast(I32),
+                    src[:, 4 * q : 4 * q + 4, :].bitcast(I32),
+                )
+            return plane
+
+        def load_table_words(src, a):
+            words = rotating([P, T], U32, "stage", 6)
+            nc.sync.dma_start(words[:].bitcast(I32), src[a].rearrange("p t i -> p (t i)").bitcast(I32))
+            return words
+
+        def interleaved_tile(cols):
+            return rotating([P, 4 * cols], BF16, "interleaved", 3)
+
+        def bank_tile():
+            return psum.tile([P, BANK], F32, name="bank", tag="bank")
+
+        def quantize(codes, plane, grouped):
+            nc.vector.quantize_mx(out=codes.bitcast(E4M3), scales=plane, in_=grouped)
+
+        def copy_on(engine, dst, src):
+            if engine == "vector":
+                nc.vector.tensor_copy(dst, src)
+            else:
+                nc.scalar.copy(dst, src)
+
+        def load_rows(src, a, c0, tag="stage", bufs=6):
+            raw = rotating([P, 4, BANK], F32, tag, bufs)
+            nc.sync.dma_start(
+                raw[:], src[BANK * a : BANK * (a + 1), c0 : c0 + BANK].rearrange("(p i) c -> p i c", i=4)
+            )
+            return raw
+
+        def load_per_row(src, name):
+            tile = held([P, 8], F32, name)
+            nc.sync.dma_start(tile[:].rearrange("p (b t) -> p b t", t=4), src.rearrange("(b p t) -> p b t", p=P, t=4))
+            return tile
+
+        def load_columns(src, rows, cols, name):
+            tile = held([P, cols.stop - cols.start], F32, name)
+            nc.sync.dma_start(tile[:], src[rows, cols])
+            return tile
+
+        offs_t = load_list(offs, "offs_t")
+        tab_plane = load_packed_scales(tab_scales, "tab_plane", nc.gpsimd, nc.sync)
+        tab_w = [load_table_words(tab_words, a) for a in range(PASSES)]
+        offs2_t = load_list(offs2, "offs2_t")
+        pos1_t = load_list(pos1, "pos1_t")
+        b1_t = load_per_row(b1, "b1_t")
+        g1_t = load_per_row(g1, "g1_t")
+        w1_raw = {}
+        w1_raw[0, 0] = load_rows(w1, 0, 0)
+        w1_raw[0, 1] = load_rows(w1, 1, 0)
+        tab2_plane = load_packed_scales(tab2_scales, "tab2_plane", nc.gpsimd, nc.sync)
+        tab2_w = [load_table_words(tab2_words, 0)]
+        w1_raw[1, 0] = load_rows(w1, 0, BANK)
+
+        v_words = []
+        for a in range(PASSES):
+            v_words.append(rotating([P, S], U32, "moving_words", 2))
+            nc.vector.tensor_copy(v_words[a][:], tab_w[a][:].indirect(offs_t[:]))
+        v_plane = held([P, S], U8, "v_plane")
+        nc.vector.tensor_copy(v_plane[:], tab_plane[:].indirect(offs_t[:]))
+
+        w1_raw[1, 1] = load_rows(w1, 1, BANK)
+        tab2_w.append(load_table_words(tab2_words, 1))
+        w2_raw = rotating([P, PASSES, H], U32, "stage", 6)
+        nc.sync.dma_start(w2_raw[:].bitcast(I32), w2_words.rearrange("a p c i -> p a (c i)").bitcast(I32))
+        w2_plane_raw = load_packed_scales(w2_scales, "w2_plane_raw", nc.gpsimd, nc.sync)
+
+        w1_codes, w1_plane = {}, {}
+
+        def quantize_w1(b, a, shares, grouped):
+            dst = grouped[:].rearrange("p (t m i) -> p m i t", t=4, i=4)
+            src = w1_raw[b, a][:].rearrange("p i (m t) -> p m i t", t=4)
+            for engine, m0, m1 in shares:
+                copy_on(engine, dst[:, m0:m1], src[:, m0:m1])
+            w1_codes[b, a] = rotating([P, BANK], U32, "dealt_words", 4)
+            w1_plane[b, a] = held([P, BANK], U8, "w1_plane%d%d" % (b, a))
+            quantize(w1_codes[b, a][:], w1_plane[b, a][:], grouped[:])
+
+        h1 = {}
+
+        def first_stage(b):
+            banks = {}
+            for t in range(4):
+                cols = slice(P * t, P * (t + 1))
+                for half in range(2):
+                    entries = slice(BANK * half, BANK * (half + 1))
+                    banks[t, half] = bank_tile()
+                    for a in range(PASSES):
+                        nc.tensor.matmul_mx(
+                            out=banks[t, half][:],
+                            lhsT=w1_codes[b, a][:, cols].bitcast(E4M3), lhsT_scale=w1_plane[b, a][:, cols],
+                            rhs=v_words[a][:, entries].bitcast(E4M3), rhs_scale=v_plane[4 * a :, entries],
+                            start=(a == 0), stop=(a == PASSES - 1),
+                        )
+            for t in range(4):
+                h1[b, t] = held([P, S], F32, "h1_%d%d" % (b, t))
+                for half in range(2):
+                    nc.scalar.activation(
+                        h1[b, t][:, BANK * half : BANK * (half + 1)], banks[t, half][:], ACT.Identity,
+                        bias=b1_t[:, 4 * b + t : 4 * b + t + 1],
+                    )
+
+        anchors = []
+
+        def pick_anchors(b):
+            anchors.append(rotating([P, 4, L], F32, "anchors%d" % b, 1))
+            for t in range(4):
+                nc.vector.tensor_copy(anchors[b][:, t, :], h1[b, t][:].indirect(pos1_t[:]))
+
+        def quantize_rows(raw, engine, name):
+            grouped = rotating([P, 4 * BANK], BF16, "stage", 6)
+            copy_on(
+                engine,
+                grouped[:].rearrange("p (c i t) -> p c t i", i=4, t=4),
+                raw[:].rearrange("p t (c i) -> p c t i", i=4),
+            )
+            codes = held([P, BANK], U32, name + "_codes")
+            plane = held([P, BANK], U8, name + "_plane")
+            quantize(codes[:], plane[:], grouped[:])
+            return codes, plane
+
+        quantize_w1(0, 0, [("scalar", 0, 128)], interleaved_tile(BANK))
+        quantize_w1(0, 1, [("vector", 0, 80), ("scalar", 80, 128)], interleaved_tile(BANK))
+        first_stage(0)
+        v2_words = []
+        for a in range(PASSES):
+            v2_words.append(held([P, L], U32, "v2_words%d" % a))
+            nc.vector.tensor_copy(v2_words[a][:], tab2_w[a][:].indirect(offs2_t[:]))
+        v2_plane = held([P, L], U8, "v2_plane")
+        nc.vector.tensor_copy(v2_plane[:], tab2_plane[:].indirect(offs2_t[:]))
+        quantize_w1(1, 0, [("vector", 0, 128)], interleaved_tile(BANK))
+        quantize_w1(1, 1, [("vector", 0, 128)], rotating([P, 4 * BANK], BF16, "anchors0", 1))
+        pick_anchors(0)
+        first_stage(1)
+
+        w5_raw = [load_rows(w5, a, 0) for a in range(PASSES)]
+        w4_raw = [load_rows(w4, 0, 0), load_rows(w4, 1, 0, "w4_last", 1)]
+        offs4_t = load_list(offs4, "offs4_t")
+        wg2_t = load_columns(wg2, slice(0, P), slice(0, L), "wg2_t")
+        pages = [load_columns(page1, slice(P * n, P * (n + 1)), slice(0, T2), "page%d" % n) for n in range(2)]
+        w3_w = held([P, PASSES, 2 * N], U8, "w3_w")
+        nc.sync.dma_start(w3_w[:].bitcast(I32), w3_words.rearrange("a p c -> p a c").bitcast(I32))
+        w3_plane = held([P, PASSES, N], U8, "w3_plane")
+        nc.gpsimd.memset(w3_plane[:].bitcast(I32), 0)
+        for q in range(4):
+            nc.sync.dma_start(
+                w3_plane[32 * q : 32 * q + 4].bitcast(I32),
+                w3_scales[:, 4 * q : 4 * q + 4, :].rearrange("a r c -> r a c").bitcast(I32),
+            )
+        offs3_t = load_list(offs3, "offs3_t")
+        wg1_t = load_columns(wg1, slice(0, P), slice(0, S), "wg1_t")
+        pages.extend([load_columns(page1, slice(P * n, P * (n + 1)), slice(0, T2), "page%d" % n) for n in range(2, 4)])
+
+        w2_plane = held([P, H], U8, "w2_plane")
+        nc.vector.tensor_copy(
+            w2_plane[:].rearrange("p (b t m) -> p b m t", b=2, t=4),
+            w2_plane_raw[:].rearrange("p (b m t) -> p b m t", b=2, t=4),
+        )
+        z2_codes, z2_plane = [], []
+
+        w2_codes = {}
+        for b in range(2):
+            for a in range(PASSES):
+                w2_codes[b, a] = rotating([P, BANK], U32, "dealt_words", 4)
+                nc.vector.tensor_copy(
+                    w2_codes[b, a][:].bitcast(I32).rearrange("p (t m) -> p m t", t=4),
+                    w2_raw[:, a, BANK * b : BANK * (b + 1)].bitcast(I32).rearrange("p (m t) -> p m t", t=4),
+                )
+
+        def make_z2(b):
+            grouped = rotating([P, 4 * L], BF16, "moving_words", 2)
+            for quarter in range(4):
+                lots = slice(P * quarter, P * (quarter + 1))
+                bank = bank_tile()
+                for t in range(4):
+                    for a in range(PASSES):
+                        nc.tensor.matmul_mx(
+                            out=bank[:, P * t : P * (t + 1)],
+                            lhsT=w2_codes[b, a][:, P * t : P * (t + 1)].bitcast(E4M3),
+                            lhsT_scale=w2_plane[4 * a :, BANK * b + P * t : BANK * b + P * (t + 1)],
+                            rhs=v2_words[a][:, lots].bitcast(E4M3), rhs_scale=v2_plane[4 * a :, lots],
+                            start=(a == 0), stop=(a == PASSES - 1),
+                        )
+                nc.vector.tensor_tensor(
+                    grouped[:, BANK * quarter : BANK * (quarter + 1)].rearrange("p (c i t) -> p c t i", i=4, t=4),
+                    bank[:].rearrange("p (t c i) -> p c t i", t=4, i=4),
+                    anchors[b][:, :, lots].rearrange("p t (c i) -> p c t i", i=4),
+                    MULT,
+                )
+            z2_codes.append(rotating([P, L], U32, "dealt_words", 4))
+            z2_plane.append(held([P, L], U8, "z2_plane%d" % b))
+            quantize(z2_codes[b][:], z2_plane[b][:], grouped[:])
+
+        z1_codes = [held([P, S], U32, "z1_codes%d" % b) for b in range(2)]
+        z1_plane = [held([P, S], U8, "z1_plane%d" % b) for b in range(2)]
+
+        def make_z1(b, c0, cols, tag, bufs):
+            entries = slice(c0, c0 + cols)
+            rounded = rotating([P, 4, cols], BF16, tag, bufs)
+            for t in range(4):
+                sine = rotating([P, cols], F32, "sines", 3)
+                nc.scalar.activation(sine[:], h1[b, t][:, entries], ACT.Sin)
+                nc.scalar.activation(
+                    rounded[:, t, :], sine[:], ACT.Copy, scale=g1_t[:, 4 * b + t : 4 * b + t + 1]
+                )
+            grouped = interleaved_tile(cols)
+            nc.scalar.copy(
+                grouped[:].rearrange("p (c i t) -> p c t i", i=4, t=4),
+                rounded[:].rearrange("p t (c i) -> p c t i", i=4),
+            )
+            quantize(z1_codes[b][:, entries], z1_plane[b][:, entries], grouped[:])
+
+        def lot_scores(tiles, tag):
+            y = rotating([P, len(tiles), L], F32, tag, 1)
+            for k, n in enumerate(tiles):
+                bank = bank_tile()
+                cols = slice(P * n, P * (n + 1))
+                for a in range(PASSES):
+                    codes, plane = w5_q[a]
+                    nc.tensor.matmul_mx(
+                        out=bank[:], lhsT=codes[:, cols].bitcast(E4M3), lhsT_scale=plane[:, cols],
+                        rhs=z2_codes[a][:].bitcast(E4M3), rhs_scale=z2_plane[a][:],
+                        start=(a == 0), stop=(a == PASSES - 1),
+                    )
+                nc.scalar.copy(y[:, k, :], bank[:])
+                nc.vector.tensor_tensor(pages[n][:].indirect(offs4_t[:]), y[:, k, :], wg2_t[:], MULT)
+
+        def item_scores(tiles, c0, cols, y4):
+            bank4, bank3 = bank_tile(), bank_tile()
+            entries = slice(c0, c0 + cols)
+            for k, n in enumerate(tiles):
+                for a in range(PASSES):
+                    codes, plane = w4_q[a]
+                    nc.tensor.matmul_mx(
+                        out=bank4[:, k * cols : (k + 1) * cols],
+                        lhsT=codes[:, P * n : P * (n + 1)].bitcast(E4M3), lhsT_scale=plane[:, P * n : P * (n + 1)],
+                        rhs=z1_codes[a][:, entries].bitcast(E4M3), rhs_scale=z1_plane[a][:, entries],
+                        start=(a == 0), stop=(a == PASSES - 1),
+                    )
+            for k, n in enumerate(tiles):
+                for a in range(PASSES):
+                    nc.tensor.matmul_mx(
+                        out=bank3[:, k * cols : (k + 1) * cols],
+                        lhsT=w3_w[:, a, 2 * P * n : 2 * P * (n + 1)].bitcast(E2M1),
+                        lhsT_scale=w3_plane[:, a, P * n : P * (n + 1)],
+                        rhs=z1_codes[a][:, entries].bitcast(E4M3), rhs_scale=z1_plane[a][:, entries],
+                        start=(a == 0), stop=(a == PASSES - 1),
+                    )
+            nc.scalar.copy(y4, bank4[:])
+            y = rotating([P, BANK], F32, "y", 2)
+            nc.vector.tensor_tensor(y[:], bank3[:], y4, MAX)
+            for k, n in enumerate(tiles):
+                nc.vector.tensor_tensor(
+                    pages[n][:].indirect(offs3_t[:, c0 // 16 : (c0 + cols) // 16]),
+                    y[:, k * cols : (k + 1) * cols], wg1_t[:, entries], MULT,
+                )
+
+        def quarter_scores(c0, tag):
+            y4 = rotating([P, 2, BANK], F32, tag, 1)
+            for h in range(2):
+                item_scores([2 * h, 2 * h + 1], c0, 256, y4[:, h, :])
+
+        make_z2(0)
+        pick_anchors(1)
+        w5_q = [quantize_rows(w5_raw[a], "scalar", "w5_%d" % a) for a in range(PASSES)]
+        make_z2(1)
+        for b in range(2):
+            make_z1(b, 0, 256, "rounded", 2)
+        w4_q = [quantize_rows(w4_raw[a], "scalar", "w4_%d" % a) for a in range(PASSES)]
+        lot_scores([0, 1], "w4_last")
+        make_z1(0, 256, 256, "hold_a", 1)
+        quarter_scores(0, "hold_a")
+        make_z1(1, 256, 256, "hold_b", 1)
+        lot_scores([2], "hold_b")
+        make_z1(0, BANK, BANK, "hold_c", 1)
+        quarter_scores(256, "hold_c")
+        make_z1(1, BANK, BANK, "hold_d", 1)
+        lot_scores([3], "hold_d")
+        for n in range(4):
+            item_scores([n], BANK, BANK, rotating([P, BANK], F32, "rounded", 2)[:])
+            nc.sync.dma_start(out[P * n : P * (n + 1), :], pages[n][:])

@@ -31,7 +31,7 @@ def tile_list_resale_disposition_slots_kernel(
         lists = ctx.enter_context(tc.tile_pool(name="lists", bufs=1))
         keep = ctx.enter_context(tc.tile_pool(name="keep", bufs=1))
         work = ctx.enter_context(tc.tile_pool(name="work", bufs=2))
-        psum = ctx.enter_context(tc.psum_pool(name="psum", bufs=8))
+        psum = ctx.enter_context(tc.psum_pool(name="psum", bufs=4))
 
         def held(shape, dtype, name):
             return keep.tile(shape, dtype, name=name, align_bytes=64)
@@ -56,15 +56,15 @@ def tile_list_resale_disposition_slots_kernel(
             return plane
 
         def load_table_words(src, a):
-            words = rotating([P, T], U32, "stage", 6)
+            words = rotating([P, T], U32, "stage", 5)
             nc.sync.dma_start(words[:].bitcast(I32), src[a].rearrange("p t i -> p (t i)").bitcast(I32))
             return words
 
         def interleaved_tile(cols):
             return rotating([P, 4 * cols], BF16, "interleaved", 3)
 
-        def bank_tile():
-            return psum.tile([P, BANK], F32, name="bank", tag="bank")
+        def bank_tile(ring):
+            return psum.tile([P, BANK], F32, name=ring, tag=ring)
 
         def quantize(codes, plane, grouped):
             nc.vector.quantize_mx(out=codes.bitcast(E4M3), scales=plane, in_=grouped)
@@ -75,7 +75,7 @@ def tile_list_resale_disposition_slots_kernel(
             else:
                 nc.scalar.copy(dst, src)
 
-        def load_rows(src, a, c0, tag="stage", bufs=6):
+        def load_rows(src, a, c0, tag="stage", bufs=5):
             raw = rotating([P, 4, BANK], F32, tag, bufs)
             nc.sync.dma_start(
                 raw[:], src[BANK * a : BANK * (a + 1), c0 : c0 + BANK].rearrange("(p i) c -> p i c", i=4)
@@ -91,6 +91,9 @@ def tile_list_resale_disposition_slots_kernel(
             tile = held([P, cols.stop - cols.start], F32, name)
             nc.sync.dma_start(tile[:], src[rows, cols])
             return tile
+
+        def load_page(n):
+            return load_columns(page1, slice(P * n, P * (n + 1)), slice(0, T2), "page%d" % n)
 
         offs_t = load_list(offs, "offs_t")
         tab_plane = load_packed_scales(tab_scales, "tab_plane", nc.gpsimd, nc.sync)
@@ -108,14 +111,14 @@ def tile_list_resale_disposition_slots_kernel(
 
         v_words = []
         for a in range(PASSES):
-            v_words.append(rotating([P, S], U32, "moving_words", 2))
+            v_words.append(rotating([P, S], U32, "moving%d" % a, 1))
             nc.vector.tensor_copy(v_words[a][:], tab_w[a][:].indirect(offs_t[:]))
         v_plane = held([P, S], U8, "v_plane")
         nc.vector.tensor_copy(v_plane[:], tab_plane[:].indirect(offs_t[:]))
 
         w1_raw[1, 1] = load_rows(w1, 1, BANK)
         tab2_w.append(load_table_words(tab2_words, 1))
-        w2_raw = rotating([P, PASSES, H], U32, "stage", 6)
+        w2_raw = rotating([P, PASSES, H], U32, "anchors1", 1)
         nc.sync.dma_start(w2_raw[:].bitcast(I32), w2_words.rearrange("a p c i -> p a (c i)").bitcast(I32))
         w2_plane_raw = load_packed_scales(w2_scales, "w2_plane_raw", nc.gpsimd, nc.sync)
 
@@ -138,7 +141,7 @@ def tile_list_resale_disposition_slots_kernel(
                 cols = slice(P * t, P * (t + 1))
                 for half in range(2):
                     entries = slice(BANK * half, BANK * (half + 1))
-                    banks[t, half] = bank_tile()
+                    banks[t, half] = bank_tile("ring_a")
                     for a in range(PASSES):
                         nc.tensor.matmul_mx(
                             out=banks[t, half][:],
@@ -161,20 +164,17 @@ def tile_list_resale_disposition_slots_kernel(
             for t in range(4):
                 nc.vector.tensor_copy(anchors[b][:, t, :], h1[b, t][:].indirect(pos1_t[:]))
 
-        def quantize_rows(raw, engine, name):
-            grouped = rotating([P, 4 * BANK], BF16, "stage", 6)
-            copy_on(
-                engine,
+        def quantize_rows(raw, grouped, codes, name):
+            nc.scalar.copy(
                 grouped[:].rearrange("p (c i t) -> p c t i", i=4, t=4),
                 raw[:].rearrange("p t (c i) -> p c t i", i=4),
             )
-            codes = held([P, BANK], U32, name + "_codes")
-            plane = held([P, BANK], U8, name + "_plane")
-            quantize(codes[:], plane[:], grouped[:])
+            plane = held([P, BANK], U8, name)
+            quantize(codes, plane[:], grouped[:])
             return codes, plane
 
         quantize_w1(0, 0, [("scalar", 0, 128)], interleaved_tile(BANK))
-        quantize_w1(0, 1, [("vector", 0, 80), ("scalar", 80, 128)], interleaved_tile(BANK))
+        quantize_w1(0, 1, [("scalar", 0, 128)], interleaved_tile(BANK))
         first_stage(0)
         v2_words = []
         for a in range(PASSES):
@@ -187,11 +187,10 @@ def tile_list_resale_disposition_slots_kernel(
         pick_anchors(0)
         first_stage(1)
 
-        w5_raw = [load_rows(w5, a, 0) for a in range(PASSES)]
-        w4_raw = [load_rows(w4, 0, 0), load_rows(w4, 1, 0, "w4_last", 1)]
+        w5_raw = [load_rows(w5, 0, 0), load_rows(w5, 1, 0, "w5_last", 1)]
         offs4_t = load_list(offs4, "offs4_t")
         wg2_t = load_columns(wg2, slice(0, P), slice(0, L), "wg2_t")
-        pages = [load_columns(page1, slice(P * n, P * (n + 1)), slice(0, T2), "page%d" % n) for n in range(2)]
+        pages = [load_page(0), load_page(1)]
         w3_w = held([P, PASSES, 2 * N], U8, "w3_w")
         nc.sync.dma_start(w3_w[:].bitcast(I32), w3_words.rearrange("a p c -> p a c").bitcast(I32))
         w3_plane = held([P, PASSES, N], U8, "w3_plane")
@@ -203,7 +202,7 @@ def tile_list_resale_disposition_slots_kernel(
             )
         offs3_t = load_list(offs3, "offs3_t")
         wg1_t = load_columns(wg1, slice(0, P), slice(0, S), "wg1_t")
-        pages.extend([load_columns(page1, slice(P * n, P * (n + 1)), slice(0, T2), "page%d" % n) for n in range(2, 4)])
+        pages.extend([load_page(2), load_page(3)])
 
         w2_plane = held([P, H], U8, "w2_plane")
         nc.vector.tensor_copy(
@@ -212,25 +211,22 @@ def tile_list_resale_disposition_slots_kernel(
         )
         z2_codes, z2_plane = [], []
 
-        w2_codes = {}
-        for b in range(2):
-            for a in range(PASSES):
-                w2_codes[b, a] = rotating([P, BANK], U32, "dealt_words", 4)
-                nc.vector.tensor_copy(
-                    w2_codes[b, a][:].bitcast(I32).rearrange("p (t m) -> p m t", t=4),
-                    w2_raw[:, a, BANK * b : BANK * (b + 1)].bitcast(I32).rearrange("p (m t) -> p m t", t=4),
-                )
+        w2_codes = rotating([P, PASSES * H], U32, "stage", 5)
+        nc.vector.tensor_copy(
+            w2_codes[:].bitcast(I32).rearrange("p (g t m) -> p g m t", g=4, t=4),
+            w2_raw[:].bitcast(I32).rearrange("p a (b m t) -> p (a b) m t", b=2, t=4),
+        )
 
         def make_z2(b):
-            grouped = rotating([P, 4 * L], BF16, "moving_words", 2)
+            grouped = rotating([P, 4 * L], BF16, "moving%d" % b, 1)
             for quarter in range(4):
                 lots = slice(P * quarter, P * (quarter + 1))
-                bank = bank_tile()
+                bank = bank_tile("ring_b")
                 for t in range(4):
                     for a in range(PASSES):
                         nc.tensor.matmul_mx(
                             out=bank[:, P * t : P * (t + 1)],
-                            lhsT=w2_codes[b, a][:, P * t : P * (t + 1)].bitcast(E4M3),
+                            lhsT=w2_codes[:, H * a + BANK * b + P * t : H * a + BANK * b + P * (t + 1)].bitcast(E4M3),
                             lhsT_scale=w2_plane[4 * a :, BANK * b + P * t : BANK * b + P * (t + 1)],
                             rhs=v2_words[a][:, lots].bitcast(E4M3), rhs_scale=v2_plane[4 * a :, lots],
                             start=(a == 0), stop=(a == PASSES - 1),
@@ -241,95 +237,118 @@ def tile_list_resale_disposition_slots_kernel(
                     anchors[b][:, :, lots].rearrange("p t (c i) -> p c t i", i=4),
                     MULT,
                 )
-            z2_codes.append(rotating([P, L], U32, "dealt_words", 4))
+            z2_codes.append(rotating([P, L], U32, "z2_codes%d" % b, 1))
             z2_plane.append(held([P, L], U8, "z2_plane%d" % b))
             quantize(z2_codes[b][:], z2_plane[b][:], grouped[:])
 
-        z1_codes = [held([P, S], U32, "z1_codes%d" % b) for b in range(2)]
-        z1_plane = [held([P, S], U8, "z1_plane%d" % b) for b in range(2)]
+        z1_codes, z1_plane = {}, {}
 
-        def make_z1(b, c0, cols, tag, bufs):
-            entries = slice(c0, c0 + cols)
-            rounded = rotating([P, 4, cols], BF16, tag, bufs)
-            for t in range(4):
-                sine = rotating([P, cols], F32, "sines", 3)
-                nc.scalar.activation(sine[:], h1[b, t][:, entries], ACT.Sin)
-                nc.scalar.activation(
-                    rounded[:, t, :], sine[:], ACT.Copy, scale=g1_t[:, 4 * b + t : 4 * b + t + 1]
-                )
-            grouped = interleaved_tile(cols)
+        def round_z1(rounded, b, t, half, tag, bufs):
+            sine = rotating([P, BANK], F32, tag, bufs)
+            nc.scalar.activation(sine[:], h1[b, t][:, BANK * half : BANK * (half + 1)], ACT.Sin)
+            nc.scalar.activation(rounded[:, t, :], sine[:], ACT.Copy, scale=g1_t[:, 4 * b + t : 4 * b + t + 1])
+
+        def quantize_z1(rounded, b, half, grouped, codes):
             nc.scalar.copy(
                 grouped[:].rearrange("p (c i t) -> p c t i", i=4, t=4),
-                rounded[:].rearrange("p t (c i) -> p c t i", i=4),
+                rounded.rearrange("p t (c i) -> p c t i", i=4),
             )
-            quantize(z1_codes[b][:, entries], z1_plane[b][:, entries], grouped[:])
+            z1_codes[b, half] = codes
+            z1_plane[b, half] = held([P, BANK], U8, "z1_plane%d%d" % (b, half))
+            quantize(codes, z1_plane[b, half][:], grouped[:])
 
-        def lot_scores(tiles, tag):
-            y = rotating([P, len(tiles), L], F32, tag, 1)
-            for k, n in enumerate(tiles):
-                bank = bank_tile()
-                cols = slice(P * n, P * (n + 1))
-                for a in range(PASSES):
-                    codes, plane = w5_q[a]
-                    nc.tensor.matmul_mx(
-                        out=bank[:], lhsT=codes[:, cols].bitcast(E4M3), lhsT_scale=plane[:, cols],
-                        rhs=z2_codes[a][:].bitcast(E4M3), rhs_scale=z2_plane[a][:],
-                        start=(a == 0), stop=(a == PASSES - 1),
-                    )
-                nc.scalar.copy(y[:, k, :], bank[:])
-                nc.vector.tensor_tensor(pages[n][:].indirect(offs4_t[:]), y[:, k, :], wg2_t[:], MULT)
-
-        def item_scores(tiles, c0, cols, y4):
-            bank4, bank3 = bank_tile(), bank_tile()
-            entries = slice(c0, c0 + cols)
-            for k, n in enumerate(tiles):
-                for a in range(PASSES):
-                    codes, plane = w4_q[a]
-                    nc.tensor.matmul_mx(
-                        out=bank4[:, k * cols : (k + 1) * cols],
-                        lhsT=codes[:, P * n : P * (n + 1)].bitcast(E4M3), lhsT_scale=plane[:, P * n : P * (n + 1)],
-                        rhs=z1_codes[a][:, entries].bitcast(E4M3), rhs_scale=z1_plane[a][:, entries],
-                        start=(a == 0), stop=(a == PASSES - 1),
-                    )
-            for k, n in enumerate(tiles):
-                for a in range(PASSES):
-                    nc.tensor.matmul_mx(
-                        out=bank3[:, k * cols : (k + 1) * cols],
-                        lhsT=w3_w[:, a, 2 * P * n : 2 * P * (n + 1)].bitcast(E2M1),
-                        lhsT_scale=w3_plane[:, a, P * n : P * (n + 1)],
-                        rhs=z1_codes[a][:, entries].bitcast(E4M3), rhs_scale=z1_plane[a][:, entries],
-                        start=(a == 0), stop=(a == PASSES - 1),
-                    )
-            nc.scalar.copy(y4, bank4[:])
-            y = rotating([P, BANK], F32, "y", 2)
-            nc.vector.tensor_tensor(y[:], bank3[:], y4, MAX)
-            for k, n in enumerate(tiles):
-                nc.vector.tensor_tensor(
-                    pages[n][:].indirect(offs3_t[:, c0 // 16 : (c0 + cols) // 16]),
-                    y[:, k * cols : (k + 1) * cols], wg1_t[:, entries], MULT,
+        def lot_products(n):
+            bank = bank_tile("ring_a")
+            cols = slice(P * n, P * (n + 1))
+            for a in range(PASSES):
+                codes, plane = w5_q[a]
+                nc.tensor.matmul_mx(
+                    out=bank[:], lhsT=codes[:, cols].bitcast(E4M3), lhsT_scale=plane[:, cols],
+                    rhs=z2_codes[a][:].bitcast(E4M3), rhs_scale=z2_plane[a][:],
+                    start=(a == 0), stop=(a == PASSES - 1),
                 )
+            return bank
 
-        def quarter_scores(c0, tag):
-            y4 = rotating([P, 2, BANK], F32, tag, 1)
-            for h in range(2):
-                item_scores([2 * h, 2 * h + 1], c0, 256, y4[:, h, :])
+        def place_lots(n, bank, y2):
+            nc.scalar.copy(y2, bank[:])
+            nc.vector.tensor_tensor(pages[n][:].indirect(offs4_t[:]), y2, wg2_t[:], MULT)
+
+        def item_scores(n, half, y4, ring):
+            bank3, bank4 = bank_tile(ring), bank_tile(ring)
+            entries = slice(BANK * half, BANK * (half + 1))
+            cols = slice(P * n, P * (n + 1))
+            for a in range(PASSES):
+                nc.tensor.matmul_mx(
+                    out=bank3[:],
+                    lhsT=w3_w[:, a, 2 * P * n : 2 * P * (n + 1)].bitcast(E2M1), lhsT_scale=w3_plane[:, a, cols],
+                    rhs=z1_codes[a, half].bitcast(E4M3), rhs_scale=z1_plane[a, half][:],
+                    start=(a == 0), stop=(a == PASSES - 1),
+                )
+            for a in range(PASSES):
+                codes, plane = w4_q[a]
+                nc.tensor.matmul_mx(
+                    out=bank4[:], lhsT=codes[:, cols].bitcast(E4M3), lhsT_scale=plane[:, cols],
+                    rhs=z1_codes[a, half].bitcast(E4M3), rhs_scale=z1_plane[a, half][:],
+                    start=(a == 0), stop=(a == PASSES - 1),
+                )
+            nc.scalar.copy(y4[:], bank4[:])
+            y = rotating([P, BANK], F32, "y", 2)
+            nc.vector.tensor_tensor(y[:], bank3[:], y4[:], MAX)
+            nc.vector.tensor_tensor(
+                pages[n][:].indirect(offs3_t[:, 32 * half : 32 * (half + 1)]), y[:], wg1_t[:, entries], MULT
+            )
+
+        def y4_tile():
+            return rotating([P, BANK], F32, "dealt_words", 4)
+
+        def words_tile(tag):
+            return rotating([P, BANK], U32, tag, 1)[:]
 
         make_z2(0)
         pick_anchors(1)
-        w5_q = [quantize_rows(w5_raw[a], "scalar", "w5_%d" % a) for a in range(PASSES)]
+        w5_q = [
+            quantize_rows(w5_raw[a], rotating([P, 4 * BANK], BF16, "stage", 5), words_tile("w5_codes%d" % a), "w5_plane%d" % a)
+            for a in range(PASSES)
+        ]
         make_z2(1)
-        for b in range(2):
-            make_z1(b, 0, 256, "rounded", 2)
-        w4_q = [quantize_rows(w4_raw[a], "scalar", "w4_%d" % a) for a in range(PASSES)]
-        lot_scores([0, 1], "w4_last")
-        make_z1(0, 256, 256, "hold_a", 1)
-        quarter_scores(0, "hold_a")
-        make_z1(1, 256, 256, "hold_b", 1)
-        lot_scores([2], "hold_b")
-        make_z1(0, BANK, BANK, "hold_c", 1)
-        quarter_scores(256, "hold_c")
-        make_z1(1, BANK, BANK, "hold_d", 1)
-        lot_scores([3], "hold_d")
+        w4_raw = [load_rows(w4, 0, 0, "w4_first", 1), load_rows(w4, 1, 0, "w4_last", 1)]
+
+        rounded = rotating([P, 4, BANK], BF16, "w5_last", 1)
+        for t in range(4):
+            round_z1(rounded, 1, t, 0, "sines", 2)
+        quantize_z1(rounded[:], 1, 0, interleaved_tile(BANK), words_tile("anchors1"))
+
+        rounded = rotating([P, 4, BANK], BF16, "w5_last", 1)
+        round_z1(rounded, 0, 0, 0, "lot0", 1)
+        round_z1(rounded, 0, 1, 0, "lot1", 1)
+        place_lots(0, lot_products(0), rotating([P, L], F32, "lot0", 1)[:])
+        place_lots(1, lot_products(1), rotating([P, L], F32, "lot1", 1)[:])
+        round_z1(rounded, 0, 2, 0, "sines", 2)
+        round_z1(rounded, 0, 3, 0, "sines", 2)
+        third_bank = lot_products(2)
+        last_bank = lot_products(3)
+        pair = rotating([P, 2 * BANK], U32, "lot1", 1)
+        quantize_z1(rounded[:], 0, 0, rotating([P, 4 * BANK], BF16, "z2_codes1", 1), pair[:, 0:BANK])
+
+        w4_q = [quantize_rows(w4_raw[0], interleaved_tile(BANK), pair[:, BANK:], "w4_plane0")]
+        place_lots(2, third_bank, rotating([P, L], F32, "w4_first", 1)[:])
+        w4_q.append(quantize_rows(w4_raw[1], interleaved_tile(BANK), words_tile("anchors0"), "w4_plane1"))
+        shared = rotating([P, 3 * BANK], F32, "w4_last", 1)
+        place_lots(3, last_bank, shared[:, 0:L])
+        for n in range(2):
+            item_scores(n, 0, y4_tile(), "ring_b")
+
+        rounded = shared[:, L:].bitcast(BF16).rearrange("p (t c) -> p t c", t=4)
+        for t in range(4):
+            round_z1(rounded, 0, t, 1, "late_sines", 2)
+        quantize_z1(rounded, 0, 1, interleaved_tile(BANK), words_tile("moving1"))
+        item_scores(2, 0, rotating([P, BANK], F32, "w4_last", 1), "ring_a")
+        rounded = rotating([P, 4, BANK], BF16, "moving0", 1)
+        for t in range(4):
+            round_z1(rounded, 1, t, 1, "late_sines", 2)
+        quantize_z1(rounded[:], 1, 1, interleaved_tile(BANK), words_tile("z1_codes11"))
+
+        item_scores(3, 0, rotating([P, BANK], F32, "moving0", 1), "ring_a")
         for n in range(4):
-            item_scores([n], BANK, BANK, rotating([P, BANK], F32, "rounded", 2)[:])
+            item_scores(n, 1, y4_tile(), "ring_b" if n < 2 else "ring_a")
             nc.sync.dma_start(out[P * n : P * (n + 1), :], pages[n][:])

@@ -105,8 +105,8 @@ def tile_list_resale_disposition_slots_kernel(
         w1_raw = {}
         w1_raw[0, 0] = load_rows(w1, 0, 0)
         w1_raw[0, 1] = load_rows(w1, 1, 0)
-        tab2_plane = load_packed_scales(tab2_scales, "tab2_plane", nc.gpsimd, nc.sync)
         tab2_w = [load_table_words(tab2_words, 0)]
+        tab2_plane = load_packed_scales(tab2_scales, "tab2_plane", nc.gpsimd, nc.sync)
         w1_raw[1, 0] = load_rows(w1, 0, BANK)
 
         v_words = []
@@ -157,6 +157,11 @@ def tile_list_resale_disposition_slots_kernel(
                         bias=b1_t[:, 4 * b + t : 4 * b + t + 1],
                     )
 
+        def round_z1(rounded, b, t, half, tag, bufs):
+            sine = rotating([P, BANK], F32, tag, bufs)
+            nc.scalar.activation(sine[:], h1[b, t][:, BANK * half : BANK * (half + 1)], ACT.Sin)
+            nc.scalar.activation(rounded[:, t, :], sine[:], ACT.Copy, scale=g1_t[:, 4 * b + t : 4 * b + t + 1])
+
         anchors = []
 
         def pick_anchors(b):
@@ -174,7 +179,7 @@ def tile_list_resale_disposition_slots_kernel(
             return codes, plane
 
         quantize_w1(0, 0, [("scalar", 0, 128)], interleaved_tile(BANK))
-        quantize_w1(0, 1, [("scalar", 0, 128)], interleaved_tile(BANK))
+        quantize_w1(0, 1, [("scalar", 0, 64), ("vector", 64, 128)], interleaved_tile(BANK))
         first_stage(0)
         v2_words = []
         for a in range(PASSES):
@@ -182,9 +187,12 @@ def tile_list_resale_disposition_slots_kernel(
             nc.vector.tensor_copy(v2_words[a][:], tab2_w[a][:].indirect(offs2_t[:]))
         v2_plane = held([P, L], U8, "v2_plane")
         nc.vector.tensor_copy(v2_plane[:], tab2_plane[:].indirect(offs2_t[:]))
-        quantize_w1(1, 0, [("vector", 0, 128)], interleaved_tile(BANK))
-        quantize_w1(1, 1, [("vector", 0, 128)], rotating([P, 4 * BANK], BF16, "anchors0", 1))
         pick_anchors(0)
+        quantize_w1(1, 0, [("vector", 0, 128)], interleaved_tile(BANK))
+        quantize_w1(1, 1, [("vector", 0, 128)], interleaved_tile(BANK))
+        first_rounded = held([P, 4, BANK], BF16, "first_rounded")
+        for t in range(4):
+            round_z1(first_rounded, 0, t, 0, "sines", 2)
         first_stage(1)
 
         w5_raw = [load_rows(w5, 0, 0), load_rows(w5, 1, 0, "w5_last", 1)]
@@ -202,12 +210,14 @@ def tile_list_resale_disposition_slots_kernel(
             )
         offs3_t = load_list(offs3, "offs3_t")
         wg1_t = load_columns(wg1, slice(0, P), slice(0, S), "wg1_t")
-        pages.extend([load_page(2), load_page(3)])
+        pages.append(load_page(2))
+        w4_raw = [load_rows(w4, 0, 0, "w4_first", 1), load_rows(w4, 1, 0, "w4_last", 1)]
+        pages.append(load_page(3))
 
         w2_plane = held([P, H], U8, "w2_plane")
         nc.vector.tensor_copy(
-            w2_plane[:].rearrange("p (b t m) -> p b m t", b=2, t=4),
-            w2_plane_raw[:].rearrange("p (b m t) -> p b m t", b=2, t=4),
+            w2_plane[:].rearrange("p (b t m) -> p b t m", b=2, t=4),
+            w2_plane_raw[:].rearrange("p (b m t) -> p b t m", b=2, t=4),
         )
         z2_codes, z2_plane = [], []
 
@@ -217,8 +227,7 @@ def tile_list_resale_disposition_slots_kernel(
             w2_raw[:].bitcast(I32).rearrange("p a (b m t) -> p (a b) m t", b=2, t=4),
         )
 
-        def make_z2(b):
-            grouped = rotating([P, 4 * L], BF16, "moving%d" % b, 1)
+        def make_z2(b, grouped):
             for quarter in range(4):
                 lots = slice(P * quarter, P * (quarter + 1))
                 bank = bank_tile("ring_b")
@@ -232,9 +241,9 @@ def tile_list_resale_disposition_slots_kernel(
                             start=(a == 0), stop=(a == PASSES - 1),
                         )
                 nc.vector.tensor_tensor(
-                    grouped[:, BANK * quarter : BANK * (quarter + 1)].rearrange("p (c i t) -> p c t i", i=4, t=4),
-                    bank[:].rearrange("p (t c i) -> p c t i", t=4, i=4),
-                    anchors[b][:, :, lots].rearrange("p t (c i) -> p c t i", i=4),
+                    grouped[:, BANK * quarter : BANK * (quarter + 1)].rearrange("p (c i t) -> p c t i", i=2, t=4),
+                    bank[:].rearrange("p (t c i) -> p c t i", t=4, i=2),
+                    anchors[b][:, :, lots].rearrange("p t (c i) -> p c t i", i=2),
                     MULT,
                 )
             z2_codes.append(rotating([P, L], U32, "z2_codes%d" % b, 1))
@@ -243,16 +252,14 @@ def tile_list_resale_disposition_slots_kernel(
 
         z1_codes, z1_plane = {}, {}
 
-        def round_z1(rounded, b, t, half, tag, bufs):
-            sine = rotating([P, BANK], F32, tag, bufs)
-            nc.scalar.activation(sine[:], h1[b, t][:, BANK * half : BANK * (half + 1)], ACT.Sin)
-            nc.scalar.activation(rounded[:, t, :], sine[:], ACT.Copy, scale=g1_t[:, 4 * b + t : 4 * b + t + 1])
-
-        def quantize_z1(rounded, b, half, grouped, codes):
+        def interleave_z1(rounded, grouped):
             nc.scalar.copy(
                 grouped[:].rearrange("p (c i t) -> p c t i", i=4, t=4),
                 rounded.rearrange("p t (c i) -> p c t i", i=4),
             )
+            return grouped
+
+        def quantize_z1(b, half, grouped, codes):
             z1_codes[b, half] = codes
             z1_plane[b, half] = held([P, BANK], U8, "z1_plane%d%d" % (b, half))
             quantize(codes, z1_plane[b, half][:], grouped[:])
@@ -304,49 +311,45 @@ def tile_list_resale_disposition_slots_kernel(
         def words_tile(tag):
             return rotating([P, BANK], U32, tag, 1)[:]
 
-        make_z2(0)
         pick_anchors(1)
+        make_z2(0, rotating([P, 4 * L], BF16, "stage", 5))
         w5_q = [
             quantize_rows(w5_raw[a], rotating([P, 4 * BANK], BF16, "stage", 5), words_tile("w5_codes%d" % a), "w5_plane%d" % a)
             for a in range(PASSES)
         ]
-        make_z2(1)
-        w4_raw = [load_rows(w4, 0, 0, "w4_first", 1), load_rows(w4, 1, 0, "w4_last", 1)]
+        make_z2(1, rotating([P, 4 * L], BF16, "moving1", 1))
+        halves = rotating([P, 2, 4 * BANK], BF16, "w5_last", 1)
+        quantize_z1(0, 0, interleave_z1(first_rounded[:], halves[:, 0, :]), words_tile("moving1"))
 
-        rounded = rotating([P, 4, BANK], BF16, "w5_last", 1)
-        for t in range(4):
-            round_z1(rounded, 1, t, 0, "sines", 2)
-        quantize_z1(rounded[:], 1, 0, interleaved_tile(BANK), words_tile("anchors1"))
-
-        rounded = rotating([P, 4, BANK], BF16, "w5_last", 1)
-        round_z1(rounded, 0, 0, 0, "lot0", 1)
-        round_z1(rounded, 0, 1, 0, "lot1", 1)
+        rounded = halves[:, 1, :].rearrange("p (t c) -> p t c", t=4)
+        round_z1(rounded, 1, 0, 0, "sines", 2)
+        round_z1(rounded, 1, 1, 0, "lot0", 1)
         place_lots(0, lot_products(0), rotating([P, L], F32, "lot0", 1)[:])
+        round_z1(rounded, 1, 2, 0, "sines", 2)
+        round_z1(rounded, 1, 3, 0, "sines", 2)
         place_lots(1, lot_products(1), rotating([P, L], F32, "lot1", 1)[:])
-        round_z1(rounded, 0, 2, 0, "sines", 2)
-        round_z1(rounded, 0, 3, 0, "sines", 2)
         third_bank = lot_products(2)
         last_bank = lot_products(3)
         pair = rotating([P, 2 * BANK], U32, "lot1", 1)
-        quantize_z1(rounded[:], 0, 0, rotating([P, 4 * BANK], BF16, "z2_codes1", 1), pair[:, 0:BANK])
+        quantize_z1(1, 0, interleave_z1(rounded, rotating([P, 4 * BANK], BF16, "z2_codes1", 1)), pair[:, 0:BANK])
 
         w4_q = [quantize_rows(w4_raw[0], interleaved_tile(BANK), pair[:, BANK:], "w4_plane0")]
         place_lots(2, third_bank, rotating([P, L], F32, "w4_first", 1)[:])
         w4_q.append(quantize_rows(w4_raw[1], interleaved_tile(BANK), words_tile("anchors0"), "w4_plane1"))
         shared = rotating([P, 3 * BANK], F32, "w4_last", 1)
         place_lots(3, last_bank, shared[:, 0:L])
-        for n in range(2):
-            item_scores(n, 0, y4_tile(), "ring_b")
 
         rounded = shared[:, L:].bitcast(BF16).rearrange("p (t c) -> p t c", t=4)
         for t in range(4):
-            round_z1(rounded, 0, t, 1, "late_sines", 2)
-        quantize_z1(rounded, 0, 1, interleaved_tile(BANK), words_tile("moving1"))
+            round_z1(rounded, 0, t, 1, "sines", 2)
+        item_scores(0, 0, rotating([P, BANK], F32, "sines", 2), "ring_b")
+        item_scores(1, 0, y4_tile(), "ring_b")
+        quantize_z1(0, 1, interleave_z1(rounded, interleaved_tile(BANK)), words_tile("anchors1"))
         item_scores(2, 0, rotating([P, BANK], F32, "w4_last", 1), "ring_a")
         rounded = rotating([P, 4, BANK], BF16, "moving0", 1)
         for t in range(4):
-            round_z1(rounded, 1, t, 1, "late_sines", 2)
-        quantize_z1(rounded[:], 1, 1, interleaved_tile(BANK), words_tile("z1_codes11"))
+            round_z1(rounded, 1, t, 1, "sines", 2)
+        quantize_z1(1, 1, interleave_z1(rounded[:], interleaved_tile(BANK)), words_tile("z1_codes11"))
 
         item_scores(3, 0, rotating([P, BANK], F32, "moving0", 1), "ring_a")
         for n in range(4):

from contextlib import ExitStack

import concourse.mybir as mybir

K, H, N, T, S, L, T2 = 1024, 1024, 512, 2048, 1024, 512, 2048
FLOPS = 2 * (K * H * S + K * H * L + 2 * H * N * S + H * N * L)

F32 = mybir.dt.float32
BF16 = mybir.dt.bfloat16
I32 = mybir.dt.int32
U32 = mybir.dt.uint32
U16 = mybir.dt.uint16
U8 = mybir.dt.uint8
E4M3 = mybir.dt.float8_e4m3fn_x4
E2M1 = mybir.dt.float4_e2m1fn_x4
ACT = mybir.ActivationFunctionType
MULT = mybir.AluOpType.mult
MAX = mybir.AluOpType.max

P = 128
PASSES = 2
BANK = 512


def tile_list_resale_disposition_slots_kernel(
    tc, tab_words, tab_scales, tab2_words, tab2_scales, offs, offs2, pos1, offs3, offs4,
    w1, b1, g1, w2_words, w2_scales, w3_words, w3_scales, w4, w5, wg1, wg2, page1, out,
):
    nc = tc.nc
    with ExitStack() as ctx:
        lists = ctx.enter_context(tc.tile_pool(name="lists", bufs=1))
        keep = ctx.enter_context(tc.tile_pool(name="keep", bufs=1))
        work = ctx.enter_context(tc.tile_pool(name="work", bufs=2))
        psum = ctx.enter_context(tc.psum_pool(name="psum", bufs=4))

        def held(shape, dtype, name):
            return keep.tile(shape, dtype, name=name, align_bytes=64)

        def rotating(shape, dtype, tag, bufs):
            return work.tile(shape, dtype, name=tag, tag=tag, bufs=bufs, align_bytes=64)

        def load_list(src, name):
            tile = lists.tile(list(src.shape), U16, name=name)
            nc.sync.dma_start(tile[:], src)
            return tile

        def load_packed_scales(src, name, clear, queue):
            cols = src.shape[2]
            plane = held([P, cols], U8, name)
            clear.memset(plane[:].bitcast(I32), 0)
            for q in range(4):
                queue.dma_start(
                    plane[32 * q : 32 * q + 4 * PASSES, :].bitcast(I32),
                    src[:, 4 * q : 4 * q + 4, :].bitcast(I32),
                )
            return plane

        def load_table_words(src, a):
            words = rotating([P, T], U32, "stage", 5)
            nc.sync.dma_start(words[:].bitcast(I32), src[a].rearrange("p t i -> p (t i)").bitcast(I32))
            return words

        def interleaved_tile(cols):
            return rotating([P, 4 * cols], BF16, "interleaved", 3)

        def bank_tile(ring):
            return psum.tile([P, BANK], F32, name=ring, tag=ring)

        def quantize(codes, plane, grouped):
            nc.vector.quantize_mx(out=codes.bitcast(E4M3), scales=plane, in_=grouped)

        def copy_on(engine, dst, src):
            if engine == "vector":
                nc.vector.tensor_copy(dst, src)
            else:
                nc.scalar.copy(dst, src)

        def load_rows(src, a, c0, tag="stage", bufs=5):
            raw = rotating([P, 4, BANK], F32, tag, bufs)
            nc.sync.dma_start(
                raw[:], src[BANK * a : BANK * (a + 1), c0 : c0 + BANK].rearrange("(p i) c -> p i c", i=4)
            )
            return raw

        def load_per_row(src, name):
            tile = held([P, 8], F32, name)
            nc.sync.dma_start(tile[:].rearrange("p (b t) -> p b t", t=4), src.rearrange("(b p t) -> p b t", p=P, t=4))
            return tile

        def load_columns(src, rows, cols, name):
            tile = held([P, cols.stop - cols.start], F32, name)
            nc.sync.dma_start(tile[:], src[rows, cols])
            return tile

        def load_page(n):
            return load_columns(page1, slice(P * n, P * (n + 1)), slice(0, T2), "page%d" % n)

        offs_t = load_list(offs, "offs_t")
        tab_plane = load_packed_scales(tab_scales, "tab_plane", nc.gpsimd, nc.sync)
        tab_w = [load_table_words(tab_words, a) for a in range(PASSES)]
        offs2_t = load_list(offs2, "offs2_t")
        pos1_t = load_list(pos1, "pos1_t")
        b1_t = load_per_row(b1, "b1_t")
        g1_t = load_per_row(g1, "g1_t")
        w1_raw = {}
        w1_raw[0, 0] = load_rows(w1, 0, 0)
        w1_raw[0, 1] = load_rows(w1, 1, 0)
        tab2_w = [load_table_words(tab2_words, 0)]
        tab2_plane = load_packed_scales(tab2_scales, "tab2_plane", nc.gpsimd, nc.sync)
        w1_raw[1, 0] = load_rows(w1, 0, BANK)

        v_words = []
        for a in range(PASSES):
            v_words.append(rotating([P, S], U32, "moving%d" % a, 1))
            nc.vector.tensor_copy(v_words[a][:], tab_w[a][:].indirect(offs_t[:]))
        v_plane = held([P, S], U8, "v_plane")
        nc.vector.tensor_copy(v_plane[:], tab_plane[:].indirect(offs_t[:]))

        w1_raw[1, 1] = load_rows(w1, 1, BANK)
        tab2_w.append(load_table_words(tab2_words, 1))
        w2_raw = rotating([P, PASSES, H], U32, "anchors1", 1)
        nc.sync.dma_start(w2_raw[:].bitcast(I32), w2_words.rearrange("a p c i -> p a (c i)").bitcast(I32))
        w2_plane_raw = load_packed_scales(w2_scales, "w2_plane_raw", nc.gpsimd, nc.sync)

        w1_codes, w1_plane = {}, {}

        def quantize_w1(b, a, shares, grouped):
            dst = grouped[:].rearrange("p (t m i) -> p m i t", t=4, i=4)
            src = w1_raw[b, a][:].rearrange("p i (m t) -> p m i t", t=4)
            for engine, m0, m1 in shares:
                copy_on(engine, dst[:, m0:m1], src[:, m0:m1])
            w1_codes[b, a] = rotating([P, BANK], U32, "dealt_words", 4)
            w1_plane[b, a] = held([P, BANK], U8, "w1_plane%d%d" % (b, a))
            quantize(w1_codes[b, a][:], w1_plane[b, a][:], grouped[:])

        h1 = {}

        def first_stage(b):
            banks = {}
            for t in range(4):
                cols = slice(P * t, P * (t + 1))
                for half in range(2):
                    entries = slice(BANK * half, BANK * (half + 1))
                    banks[t, half] = bank_tile("ring_a")
                    for a in range(PASSES):
                        nc.tensor.matmul_mx(
                            out=banks[t, half][:],
                            lhsT=w1_codes[b, a][:, cols].bitcast(E4M3), lhsT_scale=w1_plane[b, a][:, cols],
                            rhs=v_words[a][:, entries].bitcast(E4M3), rhs_scale=v_plane[4 * a :, entries],
                            start=(a == 0), stop=(a == PASSES - 1),
                        )
            for t in range(4):
                h1[b, t] = held([P, S], F32, "h1_%d%d" % (b, t))
                for half in range(2):
                    nc.scalar.activation(
                        h1[b, t][:, BANK * half : BANK * (half + 1)], banks[t, half][:], ACT.Identity,
                        bias=b1_t[:, 4 * b + t : 4 * b + t + 1],
                    )

        def round_z1(rounded, b, t, half, tag, bufs):
            sine = rotating([P, BANK], F32, tag, bufs)
            nc.scalar.activation(sine[:], h1[b, t][:, BANK * half : BANK * (half + 1)], ACT.Sin)
            nc.scalar.activation(rounded[:, t, :], sine[:], ACT.Copy, scale=g1_t[:, 4 * b + t : 4 * b + t + 1])

        anchors = []

        def pick_anchors(b):
            anchors.append(rotating([P, 4, L], F32, "anchors%d" % b, 1))
            for t in range(4):
                nc.vector.tensor_copy(anchors[b][:, t, :], h1[b, t][:].indirect(pos1_t[:]))

        def quantize_rows(raw, grouped, codes, name):
            nc.scalar.copy(
                grouped[:].rearrange("p (c i t) -> p c t i", i=4, t=4),
                raw[:].rearrange("p t (c i) -> p c t i", i=4),
            )
            plane = held([P, BANK], U8, name)
            quantize(codes, plane[:], grouped[:])
            return codes, plane

        quantize_w1(0, 0, [("scalar", 0, 128)], interleaved_tile(BANK))
        quantize_w1(0, 1, [("scalar", 0, 64), ("vector", 64, 128)], interleaved_tile(BANK))
        first_stage(0)
        v2_words = []
        for a in range(PASSES):
            v2_words.append(held([P, L], U32, "v2_words%d" % a))
            nc.vector.tensor_copy(v2_words[a][:], tab2_w[a][:].indirect(offs2_t[:]))
        v2_plane = held([P, L], U8, "v2_plane")
        nc.vector.tensor_copy(v2_plane[:], tab2_plane[:].indirect(offs2_t[:]))
        pick_anchors(0)
        quantize_w1(1, 0, [("vector", 0, 128)], interleaved_tile(BANK))
        quantize_w1(1, 1, [("vector", 0, 128)], interleaved_tile(BANK))
        first_rounded = held([P, 4, BANK], BF16, "first_rounded")
        for t in range(4):
            round_z1(first_rounded, 0, t, 0, "sines", 2)
        first_stage(1)

        w5_raw = [load_rows(w5, 0, 0), load_rows(w5, 1, 0, "w5_last", 1)]
        offs4_t = load_list(offs4, "offs4_t")
        wg2_t = load_columns(wg2, slice(0, P), slice(0, L), "wg2_t")
        pages = [load_page(0), load_page(1)]
        w3_w = held([P, PASSES, 2 * N], U8, "w3_w")
        nc.sync.dma_start(w3_w[:].bitcast(I32), w3_words.rearrange("a p c -> p a c").bitcast(I32))
        w3_plane = held([P, PASSES, N], U8, "w3_plane")
        nc.gpsimd.memset(w3_plane[:].bitcast(I32), 0)
        for q in range(4):
            nc.sync.dma_start(
                w3_plane[32 * q : 32 * q + 4].bitcast(I32),
                w3_scales[:, 4 * q : 4 * q + 4, :].rearrange("a r c -> r a c").bitcast(I32),
            )
        offs3_t = load_list(offs3, "offs3_t")
        wg1_t = load_columns(wg1, slice(0, P), slice(0, S), "wg1_t")
        pages.append(load_page(2))
        w4_raw = [load_rows(w4, 0, 0, "w4_first", 1), load_rows(w4, 1, 0, "w4_last", 1)]
        pages.append(load_page(3))

        w2_plane = held([P, H], U8, "w2_plane")
        nc.vector.tensor_copy(
            w2_plane[:].rearrange("p (b t m) -> p b t m", b=2, t=4),
            w2_plane_raw[:].rearrange("p (b m t) -> p b t m", b=2, t=4),
        )
        z2_codes, z2_plane = [], []

        w2_codes = rotating([P, PASSES * H], U32, "stage", 5)
        nc.vector.tensor_copy(
            w2_codes[:].bitcast(I32).rearrange("p (g t m) -> p g m t", g=4, t=4),
            w2_raw[:].bitcast(I32).rearrange("p a (b m t) -> p (a b) m t", b=2, t=4),
        )

        def make_z2(b, grouped):
            for quarter in range(4):
                lots = slice(P * quarter, P * (quarter + 1))
                bank = bank_tile("ring_b")
                for t in range(4):
                    for a in range(PASSES):
                        nc.tensor.matmul_mx(
                            out=bank[:, P * t : P * (t + 1)],
                            lhsT=w2_codes[:, H * a + BANK * b + P * t : H * a + BANK * b + P * (t + 1)].bitcast(E4M3),
                            lhsT_scale=w2_plane[4 * a :, BANK * b + P * t : BANK * b + P * (t + 1)],
                            rhs=v2_words[a][:, lots].bitcast(E4M3), rhs_scale=v2_plane[4 * a :, lots],
                            start=(a == 0), stop=(a == PASSES - 1),
                        )
                nc.vector.tensor_tensor(
                    grouped[:, BANK * quarter : BANK * (quarter + 1)].rearrange("p (c i t) -> p c t i", i=2, t=4),
                    bank[:].rearrange("p (t c i) -> p c t i", t=4, i=2),
                    anchors[b][:, :, lots].rearrange("p t (c i) -> p c t i", i=2),
                    MULT,
                )
            z2_codes.append(rotating([P, L], U32, "z2_codes%d" % b, 1))
            z2_plane.append(held([P, L], U8, "z2_plane%d" % b))
            quantize(z2_codes[b][:], z2_plane[b][:], grouped[:])

        z1_codes, z1_plane = {}, {}

        def interleave_z1(rounded, grouped):
            nc.scalar.copy(
                grouped[:].rearrange("p (c i t) -> p c t i", i=4, t=4),
                rounded.rearrange("p t (c i) -> p c t i", i=4),
            )
            return grouped

        def quantize_z1(b, half, grouped, codes):
            z1_codes[b, half] = codes
            z1_plane[b, half] = held([P, BANK], U8, "z1_plane%d%d" % (b, half))
            quantize(codes, z1_plane[b, half][:], grouped[:])

        def lot_products(n):
            bank = bank_tile("ring_a")
            cols = slice(P * n, P * (n + 1))
            for a in range(PASSES):
                codes, plane = w5_q[a]
                nc.tensor.matmul_mx(
                    out=bank[:], lhsT=codes[:, cols].bitcast(E4M3), lhsT_scale=plane[:, cols],
                    rhs=z2_codes[a][:].bitcast(E4M3), rhs_scale=z2_plane[a][:],
                    start=(a == 0), stop=(a == PASSES - 1),
                )
            return bank

        def place_lots(n, bank, y2):
            nc.scalar.copy(y2, bank[:])
            nc.vector.tensor_tensor(pages[n][:].indirect(offs4_t[:]), y2, wg2_t[:], MULT)

        def item_scores(n, half, y4, ring):
            bank3, bank4 = bank_tile(ring), bank_tile(ring)
            entries = slice(BANK * half, BANK * (half + 1))
            cols = slice(P * n, P * (n + 1))
            for a in range(PASSES):
                nc.tensor.matmul_mx(
                    out=bank3[:],
                    lhsT=w3_w[:, a, 2 * P * n : 2 * P * (n + 1)].bitcast(E2M1), lhsT_scale=w3_plane[:, a, cols],
                    rhs=z1_codes[a, half].bitcast(E4M3), rhs_scale=z1_plane[a, half][:],
                    start=(a == 0), stop=(a == PASSES - 1),
                )
            for a in range(PASSES):
                codes, plane = w4_q[a]
                nc.tensor.matmul_mx(
                    out=bank4[:], lhsT=codes[:, cols].bitcast(E4M3), lhsT_scale=plane[:, cols],
                    rhs=z1_codes[a, half].bitcast(E4M3), rhs_scale=z1_plane[a, half][:],
                    start=(a == 0), stop=(a == PASSES - 1),
                )
            nc.scalar.copy(y4[:], bank4[:])
            y = rotating([P, BANK], F32, "y", 2)
            nc.vector.tensor_tensor(y[:], bank3[:], y4[:], MAX)
            nc.vector.tensor_tensor(
                pages[n][:].indirect(offs3_t[:, 32 * half : 32 * (half + 1)]), y[:], wg1_t[:, entries], MULT
            )

        def y4_tile():
            return rotating([P, BANK], F32, "dealt_words", 4)

        def words_tile(tag):
            return rotating([P, BANK], U32, tag, 1)[:]

        pick_anchors(1)
        make_z2(0, rotating([P, 4 * L], BF16, "stage", 5))
        w5_q = [
            quantize_rows(w5_raw[a], rotating([P, 4 * BANK], BF16, "stage", 5), words_tile("w5_codes%d" % a), "w5_plane%d" % a)
            for a in range(PASSES)
        ]
        make_z2(1, rotating([P, 4 * L], BF16, "moving1", 1))
        halves = rotating([P, 2, 4 * BANK], BF16, "w5_last", 1)
        quantize_z1(0, 0, interleave_z1(first_rounded[:], halves[:, 0, :]), words_tile("moving1"))

        rounded = halves[:, 1, :].rearrange("p (t c) -> p t c", t=4)
        round_z1(rounded, 1, 0, 0, "sines", 2)
        round_z1(rounded, 1, 1, 0, "lot0", 1)
        place_lots(0, lot_products(0), rotating([P, L], F32, "lot0", 1)[:])
        round_z1(rounded, 1, 2, 0, "sines", 2)
        round_z1(rounded, 1, 3, 0, "sines", 2)
        place_lots(1, lot_products(1), rotating([P, L], F32, "lot1", 1)[:])
        third_bank = lot_products(2)
        last_bank = lot_products(3)
        pair = rotating([P, 2 * BANK], U32, "lot1", 1)
        quantize_z1(1, 0, interleave_z1(rounded, rotating([P, 4 * BANK], BF16, "z2_codes1", 1)), pair[:, 0:BANK])

        w4_q = [quantize_rows(w4_raw[0], interleaved_tile(BANK), pair[:, BANK:], "w4_plane0")]
        place_lots(2, third_bank, rotating([P, L], F32, "w4_first", 1)[:])
        w4_q.append(quantize_rows(w4_raw[1], interleaved_tile(BANK), words_tile("anchors0"), "w4_plane1"))
        shared = rotating([P, 3 * BANK], F32, "w4_last", 1)
        place_lots(3, last_bank, shared[:, 0:L])

        rounded = shared[:, L:].bitcast(BF16).rearrange("p (t c) -> p t c", t=4)
        for t in range(4):
            round_z1(rounded, 0, t, 1, "sines", 2)
        item_scores(0, 0, rotating([P, BANK], F32, "sines", 2), "ring_b")
        item_scores(1, 0, y4_tile(), "ring_b")
        quantize_z1(0, 1, interleave_z1(rounded, interleaved_tile(BANK)), words_tile("anchors1"))
        item_scores(2, 0, rotating([P, BANK], F32, "w4_last", 1), "ring_a")
        rounded = rotating([P, 4, BANK], BF16, "moving0", 1)
        for t in range(4):
            round_z1(rounded, 1, t, 1, "sines", 2)
        quantize_z1(1, 1, interleave_z1(rounded[:], interleaved_tile(BANK)), words_tile("z1_codes11"))

        item_scores(3, 0, rotating([P, BANK], F32, "moving0", 1), "ring_a")
        for n in range(4):
            item_scores(n, 1, y4_tile(), "ring_b" if n < 2 else "ring_a")
            nc.sync.dma_start(out[P * n : P * (n + 1), :], pages[n][:])
